import numpy as np
import ml_dtypes


def mxq(x, axis, fmt="e4m3"):
    dtype, down = {"e4m3": (ml_dtypes.float8_e4m3fn, 7), "e5m2": (ml_dtypes.float8_e5m2, 14)}[fmt]
    v = np.moveaxis(np.asarray(x, np.float32).astype(ml_dtypes.bfloat16).astype(np.float64), axis, -1)
    blocks = v.reshape(v.shape[:-1] + (-1, 32))
    amax = np.abs(blocks).max(-1, keepdims=True)
    byte = np.maximum(np.where(amax > 0, np.frexp(amax)[1] - 1 + 127, 0) - down, 1)
    scale = np.exp2(byte - 127.0)
    codes = (blocks / scale).astype(np.float32).astype(dtype).astype(np.float64)
    return np.moveaxis((codes * scale).reshape(v.shape), -1, axis)


WIDE = False


def mx_kscale(k):
    if not WIDE:
        return np.ones(k)
    levels = np.array([10, -10, 5, -5, 0])
    if k % 512:
        return np.exp2(np.random.permutation(np.resize(levels, k // 32))).repeat(32)
    a = np.empty((k // 512, 16))
    for p in range(k // 512):
        a[p, :8] = np.random.permutation(np.resize(levels, 8))
        for g in range(8):
            far = levels[np.abs(levels - a[p, g]) >= 10]
            a[p, g + 8] = far[np.random.randint(len(far))]
    return np.exp2(a.ravel()).repeat(32)


def f64(x):
    return np.asarray(x).astype(np.float64)


def striped(idx):
    return np.tile(idx.reshape(-1, 16).T, (8, 1)).astype(np.uint16)


def unstriped(offs):
    return offs[:16].T.reshape(-1).astype(np.int64)


E2M1 = np.array([0.0, 0.5, 1.0, 1.5, 2.0, 3.0, 4.0, 6.0, -0.0, -0.5, -1.0, -1.5, -2.0, -3.0, -4.0, -6.0])


def pack_weight(w, fmt):
    k, n = w.shape
    w = f64(np.asarray(w, np.float32).astype(ml_dtypes.bfloat16)).reshape(k // 32, 32, n)
    amax = np.abs(w).max(1)
    if fmt == "e4m3":
        byte = np.frexp(amax)[1] - 1 + 127 - 7
    else:
        mant, ex = np.frexp(amax / 6.0)
        byte = np.where(mant > 0.5, ex, ex - 1) + 127
    byte = np.clip(np.where(amax > 0, byte, 1), 1, 254)
    scaled = (w * np.exp2(127.0 - byte)[:, None, :]).reshape(k, n).astype(np.float32)
    by_word = np.ascontiguousarray(scaled.reshape(k // 512, 128, 4, n).transpose(0, 1, 3, 2))
    if fmt == "e4m3":
        words = by_word.astype(ml_dtypes.float8_e4m3fn).view(np.uint8)
    else:
        c = by_word.astype(ml_dtypes.float4_e2m1fn).view(np.uint8) & 0xF
        words = (c[..., 0::2] | (c[..., 1::2] << 4)).reshape(k // 512, 128, 2 * n)
    return np.ascontiguousarray(words), np.ascontiguousarray(byte.astype(np.uint8).reshape(k // 512, 16, n))


def unpack_weight(words, scales, fmt):
    g, _, n = scales.shape
    words = np.ascontiguousarray(words).reshape(g, 128, n, -1)
    if fmt == "e4m3":
        vals = words.view(ml_dtypes.float8_e4m3fn).astype(np.float64)
    else:
        nib = np.empty((g, 128, n, 4), np.uint8)
        nib[..., 0::2] = words & 0xF
        nib[..., 1::2] = words >> 4
        vals = E2M1[nib]
    vals = vals * np.repeat(np.exp2(scales.astype(np.float64) - 127.0), 8, axis=1)[..., None]
    return vals.transpose(0, 1, 3, 2).reshape(g * 512, n)


def gelu(v):
    return 0.5 * v * (1.0 + np.tanh(np.sqrt(2.0 / np.pi) * (v + 0.044715 * v**3)))


def bf(x):
    return np.asarray(x, np.float32).astype(ml_dtypes.bfloat16)


def planes(Y):
    n, m = Y.shape
    b = f64(bf(Y)).reshape(n // 32, 32, m)
    amax = np.abs(b).max(1)
    byte = np.clip(np.where(amax > 0, np.frexp(amax)[1] - 1 + 127 - 7, 1), 1, 254)
    codes = (b * np.exp2(127.0 - byte)[:, None, :]).reshape(n, m).astype(np.float32).astype(ml_dtypes.float8_e4m3fn).view(np.uint8)
    words = codes.reshape(n // 512, 128, 4, m).transpose(0, 1, 3, 2)
    return np.ascontiguousarray(words), np.ascontiguousarray(byte.astype(np.uint8).reshape(n // 512, 16, m))


K, H, N, T, S, P, P2 = 1024, 512, 1024, 4096, 2048, 1024, 512

def setup_inputs():
    n = np.random.standard_normal
    s = mx_kscale(K)[:, None]
    u = mx_kscale(H)[:, None]
    tab_words, tab_scales = pack_weight(n((K, T)) * s, "e4m3")
    w4_words, w4_scales = pack_weight(1.3 * n((H, N)) / np.sqrt(H) / u, "e2m1")
    return {
        "tab_words": tab_words, "tab_scales": tab_scales,
        "offs": striped(np.random.permutation(T)[:S]),
        "pos1": striped(np.random.permutation(S)[:P]),
        "pos2": striped(np.random.permutation(S)[:P]),
        "pos3": striped(np.random.permutation(P)[:P2]),
        "pos4": striped(np.random.permutation(S)[:P2]),
        "w1": (1.4 * n((K, H)) / np.sqrt(K) / s * u.T).astype(np.float32),
        "base": (np.exp(0.3 * n(H)) * u[:, 0]).astype(np.float32),
        "gain": (1.5 * np.exp(0.3 * n(H)) * u[:, 0]).astype(np.float32),
        "w4_words": w4_words, "w4_scales": w4_scales,
        "w3": (0.7 * n((H, N)) * np.exp(0.8 * n(N)) / np.sqrt(H) / u).astype(np.float32),
    }

def reference(tab_words, tab_scales, offs, pos1, pos2, pos3, pos4, w1, base, gain, w4_words, w4_scales, w3):
    v = unpack_weight(tab_words, tab_scales, "e4m3")[:, unstriped(offs)]
    w4 = unpack_weight(w4_words, w4_scales, "e2m1")
    h = mxq(f64(w1), 0, "e4m3").T @ v
    a1 = h[:, unstriped(pos1)] / (f64(base)[:, None] + np.abs(h[:, unstriped(pos2)]))
    a2 = np.maximum(f64(gain)[:, None] * a1[:, unstriped(pos3)], h[:, unstriped(pos4)])
    a2q = mxq(a2, 0, "e4m3")
    bent = np.tanh(w4.T @ a2q)
    y = bent + (mxq(f64(w3), 0, "e4m3").T @ a2q)
    words, scales = planes(y)
    return y, words, scales

@@ -1,0 +1,304 @@
+from contextlib import ExitStack
+
+import concourse.mybir as mybir
+
+K, H, N, T, S, PAIRS, KEPT = 1024, 512, 1024, 4096, 2048, 1024, 512
+FLOPS = 2 * K * H * S + 2 * 2 * H * N * KEPT
+
+F32 = mybir.dt.float32
+BF16 = mybir.dt.bfloat16
+I32 = mybir.dt.int32
+U32 = mybir.dt.uint32
+U16 = mybir.dt.uint16
+U8 = mybir.dt.uint8
+FP8X4 = mybir.dt.float8_e4m3fn_x4
+FP4X4 = mybir.dt.float4_e2m1fn_x4
+ACT = mybir.ActivationFunctionType
+ALU = mybir.AluOpType
+
+P = 128
+PACK = 4
+K_PASS = P * PACK
+BANK = 512
+BANKS = 8
+HALF = KEPT // 2
+LANES = 16
+
+
+def tile_list_household_linkage_features_kernel(
+    tc, tab_words, tab_scales, offs, pos1, pos2, pos3, pos4, w1, base, gain, w4_words, w4_scales, w3,
+    out_0, out_1, out_2,
+):
+    nc = tc.nc
+    with ExitStack() as ctx:
+        keep = ctx.enter_context(tc.tile_pool(name="keep", bufs=1))
+        ring = ctx.enter_context(tc.tile_pool(name="ring", bufs=2))
+        psum = ctx.enter_context(tc.psum_pool(name="psum", bufs=1))
+
+        def bank(index):
+            return psum.tile([P, BANK], F32, name="bank", tag="bank%d" % (index % BANKS))
+
+        def load_list(source, name):
+            tile = keep.tile(list(source.shape), U16, name=name)
+            nc.sync.dma_start(tile[:], source)
+            return tile
+
+        def entries(tile, first, count):
+            return tile[:, first // LANES : (first + count) // LANES]
+
+        table_scales = keep.tile([P, T], U8, name="table_scales", tag="narrow", align_bytes=64)
+        nc.vector.memset(table_scales[:].bitcast(I32), 0)
+        for q in range(4):
+            nc.gpsimd.dma_start(
+                table_scales[32 * q : 32 * q + 8, :].bitcast(I32),
+                tab_scales[:, 4 * q : 4 * q + 4, :].bitcast(I32),
+            )
+        idx = load_list(offs, "idx")
+        table_words = [keep.tile([P, T], I32, name="table_words", tag="wide%d" % a, align_bytes=64) for a in range(2)]
+
+        def load_table(a):
+            nc.sync.dma_start(table_words[a][:], tab_words[a].rearrange("p t i -> p (t i)").bitcast(I32))
+
+        def load_rows(tile, source, first_col):
+            cols = tile.shape[2]
+            nc.sync.dma_start(
+                tile, source.rearrange("(p j) c -> p j c", j=PACK)[:, :, first_col : first_col + cols]
+            )
+
+        load_table(0)
+        w1_first = keep.tile([P, PACK, H], F32, name="w1_first", tag="w1_raw")
+        load_rows(w1_first[:], w1[0:K_PASS, :], 0)
+        load_table(1)
+        base_t = keep.tile([P, PACK], F32, name="base_t")
+        nc.sync.dma_start(base_t[:], base.rearrange("(p t) -> p t", t=PACK))
+        p2 = load_list(pos2, "p2")
+        p4 = load_list(pos4, "p4")
+        p1 = load_list(pos1, "p1")
+        p3 = load_list(pos3, "p3")
+        gain_t = keep.tile([P, PACK], F32, name="gain_t")
+        nc.sync.dma_start(gain_t[:], gain.rearrange("(p t) -> p t", t=PACK))
+        w4_raw_scales = keep.tile([P, N], U8, name="w4_raw_scales")
+        nc.vector.memset(w4_raw_scales[:].bitcast(I32), 0)
+        for q in range(4):
+            nc.gpsimd.dma_start(
+                w4_raw_scales[32 * q : 32 * q + 4, :].bitcast(I32),
+                w4_scales[0, 4 * q : 4 * q + 4, :].bitcast(I32),
+            )
+
+        root = keep.tile([P, PACK], F32, name="root")
+        nc.scalar.activation(root[:], base_t[:], ACT.Abs_reciprocal_sqrt)
+        per_base = keep.tile([P, PACK], F32, name="per_base")
+        nc.scalar.activation(per_base[:], root[:], ACT.Square)
+
+        def deal_and_round(raw, grouped, first_m):
+            cols = raw.shape[2]
+            nc.scalar.copy(
+                grouped[:].rearrange("p (t m j) -> p m j t", t=PACK, j=PACK)[:, first_m : first_m + cols // PACK],
+                raw.rearrange("p j (m t) -> p m j t", t=PACK),
+            )
+
+        def quantize(grouped, name):
+            width = grouped.shape[1] // PACK
+            codes = keep.tile([P, width], U32, name=name + "_codes", align_bytes=64)
+            scales = keep.tile([P, width], U8, name=name + "_scales", align_bytes=64)
+            nc.vector.quantize_mx(out=codes[:].bitcast(FP8X4), scales=scales[:], in_=grouped[:])
+            return codes, scales
+
+        v_scales = keep.tile([P, S], U8, name="v_scales", align_bytes=64)
+        v_words = {}
+        nc.vector.tensor_copy(v_scales[:], table_scales[:].indirect(idx[:]))
+
+        def gather_words(a, first_chunk, chunks, tag):
+            tile = keep.tile([P, chunks * BANK], U32, name="v_words", tag=tag, align_bytes=64)
+            nc.vector.tensor_copy(
+                tile[:], table_words[a][:].bitcast(U32).indirect(entries(idx, first_chunk * BANK, chunks * BANK))
+            )
+            for c in range(chunks):
+                v_words[a, first_chunk + c] = tile[:, c * BANK : (c + 1) * BANK]
+
+        gather_words(0, 0, 4, "v0")
+        w1_q = []
+        grouped = keep.tile([P, PACK * K_PASS], BF16, name="grouped", tag="grouped0", align_bytes=64)
+        deal_and_round(w1_first[:], grouped, 0)
+        w1_q.append(quantize(grouped, "w1_0"))
+        gather_words(1, 0, 3, "narrow")
+        grouped = keep.tile([P, PACK * K_PASS], BF16, name="grouped", tag="grouped1", align_bytes=64)
+        w1_second = keep.tile([P, PACK, H], F32, name="w1_second", tag="w1_raw")
+        for u in range(2):
+            part = w1_second[:, :, u * H // 2 : (u + 1) * H // 2]
+            load_rows(part, w1[K_PASS:K, :], u * H // 2)
+            deal_and_round(part, grouped, u * P // 2)
+        w1_q.append(quantize(grouped, "w1_1"))
+        gather_words(1, 3, 1, "grouped1")
+        w4_raw = keep.tile([P, 2 * N], U8, name="w4_raw", tag="grouped0", align_bytes=64)
+        nc.sync.dma_start(w4_raw[:].bitcast(I32), w4_words[0].bitcast(I32))
+        w3_raw = keep.tile([P, PACK, N], F32, name="w3_raw", tag="w1_raw")
+        for g in range(2):
+            load_rows(w3_raw[:, :, g * K_PASS : (g + 1) * K_PASS], w3, g * K_PASS)
+
+        w4_codes = keep.tile([P, 2 * N], U8, name="w4_codes", align_bytes=64)
+        w4_sc = keep.tile([P, N], U8, name="w4_sc", tag="wide1", align_bytes=64)
+
+        def deal_w4():
+            nc.scalar.copy(
+                w4_codes[:].bitcast(U16).rearrange("p (g t m) -> p g m t", g=2, t=PACK),
+                w4_raw[:].bitcast(U16).rearrange("p (g m t) -> p g m t", g=2, t=PACK),
+            )
+            nc.vector.tensor_copy(
+                w4_sc[:].rearrange("p (g t m) -> p g t m", g=2, t=PACK),
+                w4_raw_scales[:].rearrange("p (g m t) -> p g t m", g=2, t=PACK),
+            )
+
+        h = [keep.tile([P, S], F32, name="h%d" % t) for t in range(PACK)]
+        a1 = [keep.tile([P, PAIRS], F32, name="a1_%d" % t) for t in range(PACK)]
+        neighbour = [keep.tile([P, KEPT], F32, name="neighbour%d" % t) for t in range(PACK)]
+
+        def features(t):
+            for c in range(S // BANK):
+                acc = bank(t * (S // BANK) + c)
+                cols = slice(c * BANK, (c + 1) * BANK)
+                for a in range(2):
+                    codes, scales = w1_q[a]
+                    nc.tensor.matmul_mx(
+                        out=acc[:],
+                        lhsT=codes[:, t * P : (t + 1) * P].bitcast(FP8X4),
+                        lhsT_scale=scales[:, t * P : (t + 1) * P],
+                        rhs=v_words[a, c].bitcast(FP8X4),
+                        rhs_scale=v_scales[4 * a :, cols],
+                        start=(a == 0),
+                        stop=(a == 1),
+                    )
+                nc.scalar.copy(h[t][:, cols], acc[:])
+
+        inverse = {}
+
+        def denominators(t):
+            d = keep.tile([P, PAIRS], F32, name="d", tag="d%d" % t, align_bytes=64)
+            halves = [d[:, u * BANK : (u + 1) * BANK] for u in range(2)]
+            for u in range(2):
+                nc.vector.tensor_copy(halves[u], h[t][:].indirect(entries(p2, u * BANK, BANK)))
+            nc.vector.tensor_copy(neighbour[t][:], h[t][:].indirect(p4[:]))
+            for part in halves:
+                nc.scalar.activation(part, part, ACT.Abs, scale=per_base[:, t : t + 1])
+            for part in halves:
+                nc.scalar.activation(part, part, ACT.Abs_reciprocal_sqrt, bias=1.0)
+            for part in halves:
+                nc.scalar.activation(part, part, ACT.Square, scale=root[:, t : t + 1])
+            inverse[t] = d
+
+        def pairs(t):
+            nc.vector.tensor_tensor(a1[t][:], h[t][:].indirect(p1[:]), inverse[t][:], ALU.mult)
+
+        def kept_rows(t, u, picked, planes):
+            nc.vector.tensor_copy(picked, a1[t][:].indirect(entries(p3, u * HALF, HALF)))
+            nc.vector.scalar_tensor_tensor(
+                planes[:, t, :], picked, gain_t[:, t : t + 1], neighbour[t][:, u * HALF : (u + 1) * HALF],
+                ALU.mult, ALU.max,
+            )
+
+        def interleave(copy, grouped_out, planes):
+            copy(
+                grouped_out[:].rearrange("p (c i t) -> p c t i", i=4, t=PACK),
+                planes[:].rearrange("p t (c i) -> p c t i", i=4),
+            )
+
+        w3_q = []
+
+        def prepare_w3(g):
+            grouped = ring.tile([P, PACK * K_PASS], BF16, name="w3_grouped", tag="w3_grouped", align_bytes=64)
+            deal_and_round(w3_raw[:, :, g * K_PASS : (g + 1) * K_PASS], grouped, 0)
+            w3_q.append(quantize(grouped, "w3_%d" % g))
+
+        features(0)
+        features(1)
+        denominators(0)
+        features(2)
+        denominators(1)
+        features(3)
+        pairs(0)
+        denominators(2)
+        deal_w4()
+        pairs(1)
+        prepare_w3(0)
+        denominators(3)
+        pairs(2)
+        prepare_w3(1)
+        pairs(3)
+
+        def kept_half(u, tags, copy):
+            planes = ring.tile([P, PACK, HALF], BF16, name="planes", tag="planes")
+            for s, tag in enumerate(tags):
+                picked = keep.tile([P, 2, HALF], F32, name="picked", tag=tag, align_bytes=64)
+                for e in range(2):
+                    kept_rows(2 * s + e, u, picked[:, e, :], planes)
+            grouped = keep.tile([P, PACK * HALF], BF16, name="a2_grouped", tag="a2_grouped%d" % u, align_bytes=64)
+            interleave(copy, grouped, planes)
+            return quantize(grouped, "a2_%d" % u)
+
+        a2_q = [
+            kept_half(0, ("d1", "d3"), nc.scalar.copy),
+            kept_half(1, ("d3", "a2_grouped0"), nc.vector.tensor_copy),
+        ]
+        y_scales = keep.tile([P, 2, KEPT], U8, name="y_scales", align_bytes=64)
+        y = {}
+
+        def second_stage(u, g):
+            a2_codes, a2_scales = a2_q[u]
+            w3_codes, w3_scales = w3_q[g]
+            y[u, g] = keep.tile([P, PACK, HALF], F32, name="y%d%d" % (u, g))
+            for s in range(2):
+                bent = bank(4 * g + 2 * s)
+                linear = bank(4 * g + 2 * s + 1)
+                for e in range(2):
+                    first = g * K_PASS + (2 * s + e) * P
+                    nc.tensor.matmul_mx(
+                        out=bent[:, e * HALF : (e + 1) * HALF],
+                        lhsT=w4_codes[:, 2 * first : 2 * (first + P)].bitcast(FP4X4),
+                        lhsT_scale=w4_sc[:, first : first + P],
+                        rhs=a2_codes[:].bitcast(FP8X4),
+                        rhs_scale=a2_scales[:],
+                        start=True,
+                        stop=True,
+                    )
+                for e in range(2):
+                    first = (2 * s + e) * P
+                    nc.tensor.matmul_mx(
+                        out=linear[:, e * HALF : (e + 1) * HALF],
+                        lhsT=w3_codes[:, first : first + P].bitcast(FP8X4),
+                        lhsT_scale=w3_scales[:, first : first + P],
+                        rhs=a2_codes[:].bitcast(FP8X4),
+                        rhs_scale=a2_scales[:],
+                        start=True,
+                        stop=True,
+                    )
+                rows = y[u, g][:, 2 * s : 2 * s + 2, :].rearrange("p t j -> p (t j)")
+                nc.scalar.activation(rows, bent[:], ACT.Tanh)
+                nc.vector.tensor_tensor(rows, rows, linear[:], ALU.add)
+            nc.sync.dma_start(
+                out_0[g * K_PASS : (g + 1) * K_PASS, :].rearrange("(p t) j -> p t j", t=PACK)[
+                    :, :, u * HALF : (u + 1) * HALF
+                ],
+                y[u, g][:],
+            )
+
+        def planes_out(u, g, copy):
+            cols = slice(u * HALF, (u + 1) * HALF)
+            grouped = ring.tile([P, PACK * HALF], BF16, name="y_grouped", tag="y_grouped", bufs=4, align_bytes=64)
+            interleave(copy, grouped, y[u, g])
+            y_codes = keep.tile([P, HALF], U32, name="y_codes%d%d" % (u, g), align_bytes=64)
+            nc.vector.quantize_mx(out=y_codes[:].bitcast(FP8X4), scales=y_scales[:, g, cols], in_=grouped[:])
+            nc.sync.dma_start(out_1[g].rearrange("p m t -> p (m t)").bitcast(I32)[:, cols], y_codes[:].bitcast(I32))
+
+        second_stage(0, 0)
+        second_stage(0, 1)
+        second_stage(1, 0)
+        planes_out(0, 0, nc.scalar.copy)
+        second_stage(1, 1)
+        planes_out(0, 1, nc.vector.tensor_copy)
+        planes_out(1, 0, nc.scalar.copy)
+        planes_out(1, 1, nc.vector.tensor_copy)
+        for q in range(4):
+            nc.scalar.dma_start(
+                out_2[:, 4 * q : 4 * q + 4, :].rearrange("g r m -> r g m").bitcast(I32),
+                y_scales[32 * q : 32 * q + 4, :, :].bitcast(I32),
+            )

@@ -32,6 +32,7 @@ def tile_list_household_linkage_features_kernel(
     nc = tc.nc
     with ExitStack() as ctx:
         keep = ctx.enter_context(tc.tile_pool(name="keep", bufs=1))
+        reused = ctx.enter_context(tc.tile_pool(name="reused", bufs=1))
         ring = ctx.enter_context(tc.tile_pool(name="ring", bufs=2))
         psum = ctx.enter_context(tc.psum_pool(name="psum", bufs=1))
 
@@ -46,7 +47,7 @@ def tile_list_household_linkage_features_kernel(
         def entries(tile, first, count):
             return tile[:, first // LANES : (first + count) // LANES]
 
-        table_scales = keep.tile([P, T], U8, name="table_scales", tag="narrow", align_bytes=64)
+        table_scales = reused.tile([P, T], U8, name="table_scales", align_bytes=64, offset=8192)
         nc.vector.memset(table_scales[:].bitcast(I32), 0)
         for q in range(4):
             nc.gpsimd.dma_start(
@@ -54,7 +55,10 @@ def tile_list_household_linkage_features_kernel(
                 tab_scales[:, 4 * q : 4 * q + 4, :].bitcast(I32),
             )
         idx = load_list(offs, "idx")
-        table_words = [keep.tile([P, T], I32, name="table_words", tag="wide%d" % a, align_bytes=64) for a in range(2)]
+        table_words = [
+            keep.tile([P, T], I32, name="table_words0"),
+            reused.tile([P, T], I32, name="table_words1", align_bytes=64, offset=16384),
+        ]
 
         def load_table(a):
             nc.sync.dma_start(table_words[a][:], tab_words[a].rearrange("p t i -> p (t i)").bitcast(I32))
@@ -66,40 +70,41 @@ def tile_list_household_linkage_features_kernel(
             )
 
         load_table(0)
-        w1_first = keep.tile([P, PACK, H], F32, name="w1_first", tag="w1_raw")
+        base_t = keep.tile([P, PACK], F32, name="base_t", tag="w1_raw")
+        nc.sync.dma_start(base_t[:], base.rearrange("(p t) -> p t", t=PACK))
+        w1_first = reused.tile([P, PACK, H], F32, name="w1_first", offset=0)
         load_rows(w1_first[:], w1[0:K_PASS, :], 0)
         load_table(1)
-        base_t = keep.tile([P, PACK], F32, name="base_t")
-        nc.sync.dma_start(base_t[:], base.rearrange("(p t) -> p t", t=PACK))
         p2 = load_list(pos2, "p2")
         p4 = load_list(pos4, "p4")
         p1 = load_list(pos1, "p1")
         p3 = load_list(pos3, "p3")
         gain_t = keep.tile([P, PACK], F32, name="gain_t")
         nc.sync.dma_start(gain_t[:], gain.rearrange("(p t) -> p t", t=PACK))
-        w4_raw_scales = keep.tile([P, N], U8, name="w4_raw_scales")
-        nc.vector.memset(w4_raw_scales[:].bitcast(I32), 0)
-        for q in range(4):
-            nc.gpsimd.dma_start(
-                w4_raw_scales[32 * q : 32 * q + 4, :].bitcast(I32),
-                w4_scales[0, 4 * q : 4 * q + 4, :].bitcast(I32),
-            )
 
         root = keep.tile([P, PACK], F32, name="root")
         nc.scalar.activation(root[:], base_t[:], ACT.Abs_reciprocal_sqrt)
         per_base = keep.tile([P, PACK], F32, name="per_base")
         nc.scalar.activation(per_base[:], root[:], ACT.Square)
 
-        def deal_and_round(raw, grouped, first_m):
+        w1_second = keep.tile([P, PACK, H], F32, name="w1_second", tag="w1_raw")
+        for u in range(2):
+            load_rows(w1_second[:, :, u * H // 2 : (u + 1) * H // 2], w1[K_PASS:K, :], u * H // 2)
+
+        def deal_and_round(copy, raw, grouped, first_m):
             cols = raw.shape[2]
-            nc.scalar.copy(
-                grouped[:].rearrange("p (t m j) -> p m j t", t=PACK, j=PACK)[:, first_m : first_m + cols // PACK],
-                raw.rearrange("p j (m t) -> p m j t", t=PACK),
+            copy(
+                grouped.rearrange("p (t m j) -> p m t j", t=PACK, j=PACK)[:, first_m : first_m + cols // PACK],
+                raw.rearrange("p j (m t) -> p m t j", t=PACK),
             )
 
-        def quantize(grouped, name):
+        def gpsimd_round(out, in_):
+            nc.gpsimd.tensor_scalar(out, in_, 1.0, 0.0, ALU.mult, ALU.add)
+
+        def quantize(grouped, name, codes=None):
             width = grouped.shape[1] // PACK
-            codes = keep.tile([P, width], U32, name=name + "_codes", align_bytes=64)
+            if codes is None:
+                codes = keep.tile([P, width], U32, name=name + "_codes", align_bytes=64)
             scales = keep.tile([P, width], U8, name=name + "_scales", align_bytes=64)
             nc.vector.quantize_mx(out=codes[:].bitcast(FP8X4), scales=scales[:], in_=grouped[:])
             return codes, scales
@@ -108,36 +113,42 @@ def tile_list_household_linkage_features_kernel(
         v_words = {}
         nc.vector.tensor_copy(v_scales[:], table_scales[:].indirect(idx[:]))
 
-        def gather_words(a, first_chunk, chunks, tag):
-            tile = keep.tile([P, chunks * BANK], U32, name="v_words", tag=tag, align_bytes=64)
+        def gather_words(a, first_chunk, chunks, tile):
             nc.vector.tensor_copy(
                 tile[:], table_words[a][:].bitcast(U32).indirect(entries(idx, first_chunk * BANK, chunks * BANK))
             )
             for c in range(chunks):
                 v_words[a, first_chunk + c] = tile[:, c * BANK : (c + 1) * BANK]
 
-        gather_words(0, 0, 4, "v0")
+        gather_words(0, 0, 4, keep.tile([P, S], U32, name="v0", align_bytes=64))
         w1_q = []
         grouped = keep.tile([P, PACK * K_PASS], BF16, name="grouped", tag="grouped0", align_bytes=64)
-        deal_and_round(w1_first[:], grouped, 0)
-        w1_q.append(quantize(grouped, "w1_0"))
-        gather_words(1, 0, 3, "narrow")
+        deal_and_round(nc.scalar.copy, w1_first[:], grouped[:], 0)
+        w1_q.append(quantize(grouped, "w1_0", reused.tile([P, H], U32, name="w1_0_codes", align_bytes=64, offset=8192)))
+        gather_words(1, 0, 3, reused.tile([P, 3 * BANK], U32, name="v1", align_bytes=64, offset=10240))
         grouped = keep.tile([P, PACK * K_PASS], BF16, name="grouped", tag="grouped1", align_bytes=64)
-        w1_second = keep.tile([P, PACK, H], F32, name="w1_second", tag="w1_raw")
         for u in range(2):
-            part = w1_second[:, :, u * H // 2 : (u + 1) * H // 2]
-            load_rows(part, w1[K_PASS:K, :], u * H // 2)
-            deal_and_round(part, grouped, u * P // 2)
+            deal_and_round(nc.scalar.copy, w1_second[:, :, u * H // 2 : (u + 1) * H // 2], grouped[:], u * P // 2)
         w1_q.append(quantize(grouped, "w1_1"))
-        gather_words(1, 3, 1, "grouped1")
-        w4_raw = keep.tile([P, 2 * N], U8, name="w4_raw", tag="grouped0", align_bytes=64)
+        gather_words(1, 3, 1, keep.tile([P, BANK], U32, name="v1_last", tag="grouped1", align_bytes=64))
+        w4_raw_scales = reused.tile([P, N], U8, name="w4_raw_scales", offset=2 * N)
+        nc.gpsimd.memset(w4_raw_scales[:].bitcast(I32), 0)
+        for q in range(4):
+            nc.sync.dma_start(
+                w4_raw_scales[32 * q : 32 * q + 4, :].bitcast(I32),
+                w4_scales[0, 4 * q : 4 * q + 4, :].bitcast(I32),
+            )
+        w4_raw = reused.tile([P, 2 * N], U8, name="w4_raw", offset=0)
         nc.sync.dma_start(w4_raw[:].bitcast(I32), w4_words[0].bitcast(I32))
-        w3_raw = keep.tile([P, PACK, N], F32, name="w3_raw", tag="w1_raw")
+        w3_raw = [
+            keep.tile([P, PACK, K_PASS], F32, name="w3_raw0", tag="w1_raw"),
+            reused.tile([P, PACK, K_PASS], F32, name="w3_raw1", align_bytes=64, offset=16384),
+        ]
         for g in range(2):
-            load_rows(w3_raw[:, :, g * K_PASS : (g + 1) * K_PASS], w3, g * K_PASS)
+            load_rows(w3_raw[g][:], w3, g * K_PASS)
 
         w4_codes = keep.tile([P, 2 * N], U8, name="w4_codes", align_bytes=64)
-        w4_sc = keep.tile([P, N], U8, name="w4_sc", tag="wide1", align_bytes=64)
+        w4_sc = reused.tile([P, N], U8, name="w4_sc", align_bytes=64, offset=24576)
 
         def deal_w4():
             nc.scalar.copy(
@@ -202,12 +213,17 @@ def tile_list_household_linkage_features_kernel(
                 planes[:].rearrange("p t (c i) -> p c t i", i=4),
             )
 
-        w3_q = []
-
-        def prepare_w3(g):
-            grouped = ring.tile([P, PACK * K_PASS], BF16, name="w3_grouped", tag="w3_grouped", align_bytes=64)
-            deal_and_round(w3_raw[:, :, g * K_PASS : (g + 1) * K_PASS], grouped, 0)
-            w3_q.append(quantize(grouped, "w3_%d" % g))
+        def prepare_w3():
+            grouped = keep.tile([P, PACK * N], BF16, name="w3_grouped", align_bytes=64)
+            for piece in range(N // P):
+                g, first_m = divmod(piece * P // PACK, P)
+                deal_and_round(
+                    gpsimd_round,
+                    w3_raw[g][:, :, first_m * PACK : first_m * PACK + P],
+                    grouped[:, g * PACK * K_PASS : (g + 1) * PACK * K_PASS],
+                    first_m,
+                )
+            return quantize(grouped, "w3", keep.tile([P, N], U32, name="w3_codes", tag="d2", align_bytes=64))
 
         features(0)
         features(1)
@@ -219,10 +235,9 @@ def tile_list_household_linkage_features_kernel(
         denominators(2)
         deal_w4()
         pairs(1)
-        prepare_w3(0)
         denominators(3)
         pairs(2)
-        prepare_w3(1)
+        w3_codes, w3_scales = prepare_w3()
         pairs(3)
 
         def kept_half(u, tags, copy):
@@ -244,7 +259,6 @@ def tile_list_household_linkage_features_kernel(
 
         def second_stage(u, g):
             a2_codes, a2_scales = a2_q[u]
-            w3_codes, w3_scales = w3_q[g]
             y[u, g] = keep.tile([P, PACK, HALF], F32, name="y%d%d" % (u, g))
             for s in range(2):
                 bent = bank(4 * g + 2 * s)
@@ -261,7 +275,7 @@ def tile_list_household_linkage_features_kernel(
                         stop=True,
                     )
                 for e in range(2):
-                    first = (2 * s + e) * P
+                    first = g * K_PASS + (2 * s + e) * P
                     nc.tensor.matmul_mx(
                         out=linear[:, e * HALF : (e + 1) * HALF],
                         lhsT=w3_codes[:, first : first + P].bitcast(FP8X4),

@@ -47,17 +47,11 @@ def tile_list_household_linkage_features_kernel(
         def entries(tile, first, count):
             return tile[:, first // LANES : (first + count) // LANES]
 
-        table_scales = reused.tile([P, T], U8, name="table_scales", align_bytes=64, offset=8192)
-        nc.vector.memset(table_scales[:].bitcast(I32), 0)
-        for q in range(4):
-            nc.gpsimd.dma_start(
-                table_scales[32 * q : 32 * q + 8, :].bitcast(I32),
-                tab_scales[:, 4 * q : 4 * q + 4, :].bitcast(I32),
-            )
         idx = load_list(offs, "idx")
+        base_t = reused.tile([P, PACK], F32, name="base_t", align_bytes=64, offset=12288)
         table_words = [
-            keep.tile([P, T], I32, name="table_words0"),
-            reused.tile([P, T], I32, name="table_words1", align_bytes=64, offset=16384),
+            reused.tile([P, T], I32, name="table_words0", align_bytes=64, offset=28672),
+            reused.tile([P, T], I32, name="table_words1", align_bytes=64, offset=12288),
         ]
 
         def load_table(a):
@@ -70,26 +64,29 @@ def tile_list_household_linkage_features_kernel(
             )
 
         load_table(0)
-        base_t = keep.tile([P, PACK], F32, name="base_t", tag="w1_raw")
         nc.sync.dma_start(base_t[:], base.rearrange("(p t) -> p t", t=PACK))
-        w1_first = reused.tile([P, PACK, H], F32, name="w1_first", offset=0)
-        load_rows(w1_first[:], w1[0:K_PASS, :], 0)
-        load_table(1)
         p2 = load_list(pos2, "p2")
         p4 = load_list(pos4, "p4")
         p1 = load_list(pos1, "p1")
         p3 = load_list(pos3, "p3")
+        w1_first = reused.tile([P, PACK, H], F32, name="w1_first", offset=0)
+        load_rows(w1_first[:], w1[0:K_PASS, :], 0)
+        table_scales = keep.tile([P, T], U8, name="table_scales")
+        nc.vector.memset(table_scales[:].bitcast(I32), 0)
+        for q in range(4):
+            nc.sync.dma_start(
+                table_scales[32 * q : 32 * q + 8, :].bitcast(I32),
+                tab_scales[:, 4 * q : 4 * q + 4, :].bitcast(I32),
+            )
         gain_t = keep.tile([P, PACK], F32, name="gain_t")
-        nc.sync.dma_start(gain_t[:], gain.rearrange("(p t) -> p t", t=PACK))
+        nc.gpsimd.dma_start(gain_t[:], gain.rearrange("(p t) -> p t", t=PACK))
 
         root = keep.tile([P, PACK], F32, name="root")
         nc.scalar.activation(root[:], base_t[:], ACT.Abs_reciprocal_sqrt)
         per_base = keep.tile([P, PACK], F32, name="per_base")
         nc.scalar.activation(per_base[:], root[:], ACT.Square)
 
-        w1_second = keep.tile([P, PACK, H], F32, name="w1_second", tag="w1_raw")
-        for u in range(2):
-            load_rows(w1_second[:, :, u * H // 2 : (u + 1) * H // 2], w1[K_PASS:K, :], u * H // 2)
+        load_table(1)
 
         def deal_and_round(copy, raw, grouped, first_m):
             cols = raw.shape[2]
@@ -101,10 +98,9 @@ def tile_list_household_linkage_features_kernel(
         def gpsimd_round(out, in_):
             nc.gpsimd.tensor_scalar(out, in_, 1.0, 0.0, ALU.mult, ALU.add)
 
-        def quantize(grouped, name, codes=None):
+        def quantize(grouped, name, codes_tag=""):
             width = grouped.shape[1] // PACK
-            if codes is None:
-                codes = keep.tile([P, width], U32, name=name + "_codes", align_bytes=64)
+            codes = keep.tile([P, width], U32, name=name + "_codes", tag=codes_tag, align_bytes=64)
             scales = keep.tile([P, width], U8, name=name + "_scales", align_bytes=64)
             nc.vector.quantize_mx(out=codes[:].bitcast(FP8X4), scales=scales[:], in_=grouped[:])
             return codes, scales
@@ -124,31 +120,34 @@ def tile_list_household_linkage_features_kernel(
         w1_q = []
         grouped = keep.tile([P, PACK * K_PASS], BF16, name="grouped", tag="grouped0", align_bytes=64)
         deal_and_round(nc.scalar.copy, w1_first[:], grouped[:], 0)
-        w1_q.append(quantize(grouped, "w1_0", reused.tile([P, H], U32, name="w1_0_codes", align_bytes=64, offset=8192)))
-        gather_words(1, 0, 3, reused.tile([P, 3 * BANK], U32, name="v1", align_bytes=64, offset=10240))
+        w1_second = reused.tile([P, PACK, H], F32, name="w1_second", align_bytes=64, offset=28672)
+        for u in range(2):
+            load_rows(w1_second[:, :, u * H // 2 : (u + 1) * H // 2], w1[K_PASS:K, :], u * H // 2)
+        w1_q.append(quantize(grouped, "w1_0"))
+        gather_words(1, 0, 3, keep.tile([P, 3 * BANK], U32, name="v1", align_bytes=64))
         grouped = keep.tile([P, PACK * K_PASS], BF16, name="grouped", tag="grouped1", align_bytes=64)
         for u in range(2):
             deal_and_round(nc.scalar.copy, w1_second[:, :, u * H // 2 : (u + 1) * H // 2], grouped[:], u * P // 2)
         w1_q.append(quantize(grouped, "w1_1"))
         gather_words(1, 3, 1, keep.tile([P, BANK], U32, name="v1_last", tag="grouped1", align_bytes=64))
-        w4_raw_scales = reused.tile([P, N], U8, name="w4_raw_scales", offset=2 * N)
+        w4_raw_scales = reused.tile([P, N], U8, name="w4_raw_scales", offset=28672 + 8192 + 2 * N)
         nc.gpsimd.memset(w4_raw_scales[:].bitcast(I32), 0)
         for q in range(4):
             nc.sync.dma_start(
                 w4_raw_scales[32 * q : 32 * q + 4, :].bitcast(I32),
                 w4_scales[0, 4 * q : 4 * q + 4, :].bitcast(I32),
             )
-        w4_raw = reused.tile([P, 2 * N], U8, name="w4_raw", offset=0)
+        w4_raw = reused.tile([P, 2 * N], U8, name="w4_raw", offset=28672 + 8192)
         nc.sync.dma_start(w4_raw[:].bitcast(I32), w4_words[0].bitcast(I32))
         w3_raw = [
-            keep.tile([P, PACK, K_PASS], F32, name="w3_raw0", tag="w1_raw"),
-            reused.tile([P, PACK, K_PASS], F32, name="w3_raw1", align_bytes=64, offset=16384),
+            reused.tile([P, PACK, K_PASS], F32, name="w3_raw0", align_bytes=64, offset=28672),
+            reused.tile([P, PACK, K_PASS], F32, name="w3_raw1", align_bytes=64, offset=12288),
         ]
         for g in range(2):
             load_rows(w3_raw[g][:], w3, g * K_PASS)
 
         w4_codes = keep.tile([P, 2 * N], U8, name="w4_codes", align_bytes=64)
-        w4_sc = reused.tile([P, N], U8, name="w4_sc", align_bytes=64, offset=24576)
+        w4_sc = reused.tile([P, N], U8, name="w4_sc", align_bytes=64, offset=20480)
 
         def deal_w4():
             nc.scalar.copy(
@@ -223,7 +222,7 @@ def tile_list_household_linkage_features_kernel(
                     grouped[:, g * PACK * K_PASS : (g + 1) * PACK * K_PASS],
                     first_m,
                 )
-            return quantize(grouped, "w3", keep.tile([P, N], U32, name="w3_codes", tag="d2", align_bytes=64))
+            return quantize(grouped, "w3", "d2")
 
         features(0)
         features(1)
@@ -241,7 +240,7 @@ def tile_list_household_linkage_features_kernel(
         pairs(3)
 
         def kept_half(u, tags, copy):
-            planes = ring.tile([P, PACK, HALF], BF16, name="planes", tag="planes")
+            planes = keep.tile([P, PACK, HALF], BF16, name="planes", tag="planes%d" % u, align_bytes=64)
             for s, tag in enumerate(tags):
                 picked = keep.tile([P, 2, HALF], F32, name="picked", tag=tag, align_bytes=64)
                 for e in range(2):
@@ -252,7 +251,7 @@ def tile_list_household_linkage_features_kernel(
 
         a2_q = [
             kept_half(0, ("d1", "d3"), nc.scalar.copy),
-            kept_half(1, ("d3", "a2_grouped0"), nc.vector.tensor_copy),
+            kept_half(1, ("d3", "planes0"), nc.vector.tensor_copy),
         ]
         y_scales = keep.tile([P, 2, KEPT], U8, name="y_scales", align_bytes=64)
         y = {}

from contextlib import ExitStack

import concourse.mybir as mybir

K, H, N, T, S, PAIRS, KEPT = 1024, 512, 1024, 4096, 2048, 1024, 512
FLOPS = 2 * K * H * S + 2 * 2 * H * N * KEPT

F32 = mybir.dt.float32
BF16 = mybir.dt.bfloat16
I32 = mybir.dt.int32
U32 = mybir.dt.uint32
U16 = mybir.dt.uint16
U8 = mybir.dt.uint8
FP8X4 = mybir.dt.float8_e4m3fn_x4
FP4X4 = mybir.dt.float4_e2m1fn_x4
ACT = mybir.ActivationFunctionType
ALU = mybir.AluOpType

P = 128
PACK = 4
K_PASS = P * PACK
BANK = 512
BANKS = 8
HALF = KEPT // 2
LANES = 16


def tile_list_household_linkage_features_kernel(
    tc, tab_words, tab_scales, offs, pos1, pos2, pos3, pos4, w1, base, gain, w4_words, w4_scales, w3,
    out_0, out_1, out_2,
):
    nc = tc.nc
    with ExitStack() as ctx:
        keep = ctx.enter_context(tc.tile_pool(name="keep", bufs=1))
        reused = ctx.enter_context(tc.tile_pool(name="reused", bufs=1))
        ring = ctx.enter_context(tc.tile_pool(name="ring", bufs=2))
        psum = ctx.enter_context(tc.psum_pool(name="psum", bufs=1))

        def bank(index):
            return psum.tile([P, BANK], F32, name="bank", tag="bank%d" % (index % BANKS))

        def load_list(source, name):
            tile = keep.tile(list(source.shape), U16, name=name)
            nc.sync.dma_start(tile[:], source)
            return tile

        def entries(tile, first, count):
            return tile[:, first // LANES : (first + count) // LANES]

        idx = load_list(offs, "idx")
        base_t = reused.tile([P, PACK], F32, name="base_t", align_bytes=64, offset=12288)
        table_words = [
            reused.tile([P, T], I32, name="table_words0", align_bytes=64, offset=28672),
            reused.tile([P, T], I32, name="table_words1", align_bytes=64, offset=12288),
        ]

        def load_table(a):
            nc.sync.dma_start(table_words[a][:], tab_words[a].rearrange("p t i -> p (t i)").bitcast(I32))

        def load_rows(tile, source, first_col):
            cols = tile.shape[2]
            nc.sync.dma_start(
                tile, source.rearrange("(p j) c -> p j c", j=PACK)[:, :, first_col : first_col + cols]
            )

        load_table(0)
        nc.sync.dma_start(base_t[:], base.rearrange("(p t) -> p t", t=PACK))
        p2 = load_list(pos2, "p2")
        p4 = load_list(pos4, "p4")
        p1 = load_list(pos1, "p1")
        p3 = load_list(pos3, "p3")
        w1_first = reused.tile([P, PACK, H], F32, name="w1_first", offset=0)
        load_rows(w1_first[:], w1[0:K_PASS, :], 0)
        table_scales = keep.tile([P, T], U8, name="table_scales")
        nc.vector.memset(table_scales[:].bitcast(I32), 0)
        for q in range(4):
            nc.sync.dma_start(
                table_scales[32 * q : 32 * q + 8, :].bitcast(I32),
                tab_scales[:, 4 * q : 4 * q + 4, :].bitcast(I32),
            )
        gain_t = keep.tile([P, PACK], F32, name="gain_t")
        nc.gpsimd.dma_start(gain_t[:], gain.rearrange("(p t) -> p t", t=PACK))

        root = keep.tile([P, PACK], F32, name="root")
        nc.scalar.activation(root[:], base_t[:], ACT.Abs_reciprocal_sqrt)
        per_base = keep.tile([P, PACK], F32, name="per_base")
        nc.scalar.activation(per_base[:], root[:], ACT.Square)

        load_table(1)

        def deal_and_round(copy, raw, grouped, first_m):
            cols = raw.shape[2]
            copy(
                grouped.rearrange("p (t m j) -> p m t j", t=PACK, j=PACK)[:, first_m : first_m + cols // PACK],
                raw.rearrange("p j (m t) -> p m t j", t=PACK),
            )

        def gpsimd_round(out, in_):
            nc.gpsimd.tensor_scalar(out, in_, 1.0, 0.0, ALU.mult, ALU.add)

        def quantize(grouped, name, codes_tag=""):
            width = grouped.shape[1] // PACK
            codes = keep.tile([P, width], U32, name=name + "_codes", tag=codes_tag, align_bytes=64)
            scales = keep.tile([P, width], U8, name=name + "_scales", align_bytes=64)
            nc.vector.quantize_mx(out=codes[:].bitcast(FP8X4), scales=scales[:], in_=grouped[:])
            return codes, scales

        v_scales = keep.tile([P, S], U8, name="v_scales", align_bytes=64)
        v_words = {}
        nc.vector.tensor_copy(v_scales[:], table_scales[:].indirect(idx[:]))

        def gather_words(a, first_chunk, chunks, tile):
            nc.vector.tensor_copy(
                tile[:], table_words[a][:].bitcast(U32).indirect(entries(idx, first_chunk * BANK, chunks * BANK))
            )
            for c in range(chunks):
                v_words[a, first_chunk + c] = tile[:, c * BANK : (c + 1) * BANK]

        gather_words(0, 0, 4, keep.tile([P, S], U32, name="v0", align_bytes=64))
        w1_q = []
        grouped = keep.tile([P, PACK * K_PASS], BF16, name="grouped", tag="grouped0", align_bytes=64)
        deal_and_round(nc.scalar.copy, w1_first[:], grouped[:], 0)
        w1_second = reused.tile([P, PACK, H], F32, name="w1_second", align_bytes=64, offset=28672)
        for u in range(2):
            load_rows(w1_second[:, :, u * H // 2 : (u + 1) * H // 2], w1[K_PASS:K, :], u * H // 2)
        w1_q.append(quantize(grouped, "w1_0"))
        gather_words(1, 0, 3, keep.tile([P, 3 * BANK], U32, name="v1", align_bytes=64))
        grouped = keep.tile([P, PACK * K_PASS], BF16, name="grouped", tag="grouped1", align_bytes=64)
        for u in range(2):
            deal_and_round(nc.scalar.copy, w1_second[:, :, u * H // 2 : (u + 1) * H // 2], grouped[:], u * P // 2)
        w1_q.append(quantize(grouped, "w1_1"))
        gather_words(1, 3, 1, keep.tile([P, BANK], U32, name="v1_last", tag="grouped1", align_bytes=64))
        w4_raw_scales = reused.tile([P, N], U8, name="w4_raw_scales", offset=28672 + 8192 + 2 * N)
        nc.gpsimd.memset(w4_raw_scales[:].bitcast(I32), 0)
        for q in range(4):
            nc.sync.dma_start(
                w4_raw_scales[32 * q : 32 * q + 4, :].bitcast(I32),
                w4_scales[0, 4 * q : 4 * q + 4, :].bitcast(I32),
            )
        w4_raw = reused.tile([P, 2 * N], U8, name="w4_raw", offset=28672 + 8192)
        nc.sync.dma_start(w4_raw[:].bitcast(I32), w4_words[0].bitcast(I32))
        w3_raw = [
            reused.tile([P, PACK, K_PASS], F32, name="w3_raw0", align_bytes=64, offset=28672),
            reused.tile([P, PACK, K_PASS], F32, name="w3_raw1", align_bytes=64, offset=12288),
        ]
        for g in range(2):
            load_rows(w3_raw[g][:], w3, g * K_PASS)

        w4_codes = keep.tile([P, 2 * N], U8, name="w4_codes", align_bytes=64)
        w4_sc = reused.tile([P, N], U8, name="w4_sc", align_bytes=64, offset=20480)

        def deal_w4():
            nc.scalar.copy(
                w4_codes[:].bitcast(U16).rearrange("p (g t m) -> p g m t", g=2, t=PACK),
                w4_raw[:].bitcast(U16).rearrange("p (g m t) -> p g m t", g=2, t=PACK),
            )
            nc.vector.tensor_copy(
                w4_sc[:].rearrange("p (g t m) -> p g t m", g=2, t=PACK),
                w4_raw_scales[:].rearrange("p (g m t) -> p g t m", g=2, t=PACK),
            )

        h = [keep.tile([P, S], F32, name="h%d" % t) for t in range(PACK)]
        a1 = [keep.tile([P, PAIRS], F32, name="a1_%d" % t) for t in range(PACK)]
        neighbour = [keep.tile([P, KEPT], F32, name="neighbour%d" % t) for t in range(PACK)]

        def features(t):
            for c in range(S // BANK):
                acc = bank(t * (S // BANK) + c)
                cols = slice(c * BANK, (c + 1) * BANK)
                for a in range(2):
                    codes, scales = w1_q[a]
                    nc.tensor.matmul_mx(
                        out=acc[:],
                        lhsT=codes[:, t * P : (t + 1) * P].bitcast(FP8X4),
                        lhsT_scale=scales[:, t * P : (t + 1) * P],
                        rhs=v_words[a, c].bitcast(FP8X4),
                        rhs_scale=v_scales[4 * a :, cols],
                        start=(a == 0),
                        stop=(a == 1),
                    )
                nc.scalar.copy(h[t][:, cols], acc[:])

        inverse = {}

        def denominators(t):
            d = keep.tile([P, PAIRS], F32, name="d", tag="d%d" % t, align_bytes=64)
            halves = [d[:, u * BANK : (u + 1) * BANK] for u in range(2)]
            for u in range(2):
                nc.vector.tensor_copy(halves[u], h[t][:].indirect(entries(p2, u * BANK, BANK)))
            nc.vector.tensor_copy(neighbour[t][:], h[t][:].indirect(p4[:]))
            for part in halves:
                nc.scalar.activation(part, part, ACT.Abs, scale=per_base[:, t : t + 1])
            for part in halves:
                nc.scalar.activation(part, part, ACT.Abs_reciprocal_sqrt, bias=1.0)
            for part in halves:
                nc.scalar.activation(part, part, ACT.Square, scale=root[:, t : t + 1])
            inverse[t] = d

        def pairs(t):
            nc.vector.tensor_tensor(a1[t][:], h[t][:].indirect(p1[:]), inverse[t][:], ALU.mult)

        def kept_rows(t, u, picked, planes):
            nc.vector.tensor_copy(picked, a1[t][:].indirect(entries(p3, u * HALF, HALF)))
            nc.vector.scalar_tensor_tensor(
                planes[:, t, :], picked, gain_t[:, t : t + 1], neighbour[t][:, u * HALF : (u + 1) * HALF],
                ALU.mult, ALU.max,
            )

        def interleave(copy, grouped_out, planes):
            copy(
                grouped_out[:].rearrange("p (c i t) -> p c t i", i=4, t=PACK),
                planes[:].rearrange("p t (c i) -> p c t i", i=4),
            )

        def prepare_w3():
            grouped = keep.tile([P, PACK * N], BF16, name="w3_grouped", align_bytes=64)
            for piece in range(N // P):
                g, first_m = divmod(piece * P // PACK, P)
                deal_and_round(
                    gpsimd_round,
                    w3_raw[g][:, :, first_m * PACK : first_m * PACK + P],
                    grouped[:, g * PACK * K_PASS : (g + 1) * PACK * K_PASS],
                    first_m,
                )
            return quantize(grouped, "w3", "d2")

        features(0)
        features(1)
        denominators(0)
        features(2)
        denominators(1)
        features(3)
        pairs(0)
        denominators(2)
        deal_w4()
        pairs(1)
        denominators(3)
        pairs(2)
        w3_codes, w3_scales = prepare_w3()
        pairs(3)

        def kept_half(u, tags, copy):
            planes = keep.tile([P, PACK, HALF], BF16, name="planes", tag="planes%d" % u, align_bytes=64)
            for s, tag in enumerate(tags):
                picked = keep.tile([P, 2, HALF], F32, name="picked", tag=tag, align_bytes=64)
                for e in range(2):
                    kept_rows(2 * s + e, u, picked[:, e, :], planes)
            grouped = keep.tile([P, PACK * HALF], BF16, name="a2_grouped", tag="a2_grouped%d" % u, align_bytes=64)
            interleave(copy, grouped, planes)
            return quantize(grouped, "a2_%d" % u)

        a2_q = [
            kept_half(0, ("d1", "d3"), nc.scalar.copy),
            kept_half(1, ("d3", "planes0"), nc.vector.tensor_copy),
        ]
        y_scales = keep.tile([P, 2, KEPT], U8, name="y_scales", align_bytes=64)
        y = {}

        def second_stage(u, g):
            a2_codes, a2_scales = a2_q[u]
            y[u, g] = keep.tile([P, PACK, HALF], F32, name="y%d%d" % (u, g))
            for s in range(2):
                bent = bank(4 * g + 2 * s)
                linear = bank(4 * g + 2 * s + 1)
                for e in range(2):
                    first = g * K_PASS + (2 * s + e) * P
                    nc.tensor.matmul_mx(
                        out=bent[:, e * HALF : (e + 1) * HALF],
                        lhsT=w4_codes[:, 2 * first : 2 * (first + P)].bitcast(FP4X4),
                        lhsT_scale=w4_sc[:, first : first + P],
                        rhs=a2_codes[:].bitcast(FP8X4),
                        rhs_scale=a2_scales[:],
                        start=True,
                        stop=True,
                    )
                for e in range(2):
                    first = g * K_PASS + (2 * s + e) * P
                    nc.tensor.matmul_mx(
                        out=linear[:, e * HALF : (e + 1) * HALF],
                        lhsT=w3_codes[:, first : first + P].bitcast(FP8X4),
                        lhsT_scale=w3_scales[:, first : first + P],
                        rhs=a2_codes[:].bitcast(FP8X4),
                        rhs_scale=a2_scales[:],
                        start=True,
                        stop=True,
                    )
                rows = y[u, g][:, 2 * s : 2 * s + 2, :].rearrange("p t j -> p (t j)")
                nc.scalar.activation(rows, bent[:], ACT.Tanh)
                nc.vector.tensor_tensor(rows, rows, linear[:], ALU.add)
            nc.sync.dma_start(
                out_0[g * K_PASS : (g + 1) * K_PASS, :].rearrange("(p t) j -> p t j", t=PACK)[
                    :, :, u * HALF : (u + 1) * HALF
                ],
                y[u, g][:],
            )

        def planes_out(u, g, copy):
            cols = slice(u * HALF, (u + 1) * HALF)
            grouped = ring.tile([P, PACK * HALF], BF16, name="y_grouped", tag="y_grouped", bufs=4, align_bytes=64)
            interleave(copy, grouped, y[u, g])
            y_codes = keep.tile([P, HALF], U32, name="y_codes%d%d" % (u, g), align_bytes=64)
            nc.vector.quantize_mx(out=y_codes[:].bitcast(FP8X4), scales=y_scales[:, g, cols], in_=grouped[:])
            nc.sync.dma_start(out_1[g].rearrange("p m t -> p (m t)").bitcast(I32)[:, cols], y_codes[:].bitcast(I32))

        second_stage(0, 0)
        second_stage(0, 1)
        second_stage(1, 0)
        planes_out(0, 0, nc.scalar.copy)
        second_stage(1, 1)
        planes_out(0, 1, nc.vector.tensor_copy)
        planes_out(1, 0, nc.scalar.copy)
        planes_out(1, 1, nc.vector.tensor_copy)
        for q in range(4):
            nc.scalar.dma_start(
                out_2[:, 4 * q : 4 * q + 4, :].rearrange("g r m -> r g m").bitcast(I32),
                y_scales[32 * q : 32 * q + 4, :, :].bitcast(I32),
            )
